import numpy as np
import ml_dtypes


def mxq(x, axis, fmt="e4m3"):
    dtype, down = {"e4m3": (ml_dtypes.float8_e4m3fn, 7), "e5m2": (ml_dtypes.float8_e5m2, 14)}[fmt]
    v = np.moveaxis(np.asarray(x, np.float32).astype(ml_dtypes.bfloat16).astype(np.float64), axis, -1)
    blocks = v.reshape(v.shape[:-1] + (-1, 32))
    amax = np.abs(blocks).max(-1, keepdims=True)
    byte = np.maximum(np.where(amax > 0, np.frexp(amax)[1] - 1 + 127, 0) - down, 1)
    scale = np.exp2(byte - 127.0)
    codes = (blocks / scale).astype(np.float32).astype(dtype).astype(np.float64)
    return np.moveaxis((codes * scale).reshape(v.shape), -1, axis)


WIDE = False


def mx_kscale(k):
    if not WIDE:
        return np.ones(k)
    levels = np.array([10, -10, 5, -5, 0])
    if k % 512:
        return np.exp2(np.random.permutation(np.resize(levels, k // 32))).repeat(32)
    a = np.empty((k // 512, 16))
    for p in range(k // 512):
        a[p, :8] = np.random.permutation(np.resize(levels, 8))
        for g in range(8):
            far = levels[np.abs(levels - a[p, g]) >= 10]
            a[p, g + 8] = far[np.random.randint(len(far))]
    return np.exp2(a.ravel()).repeat(32)


def f64(x):
    return np.asarray(x).astype(np.float64)


def striped8(idx):
    return np.concatenate([x.reshape(-1, 16).T for x in idx]).astype(np.uint16)


def runs(offs, k):
    lists = np.stack([offs[16 * r : 16 * r + 16].T.reshape(-1) for r in range(8)]).astype(np.int64)
    return lists[np.arange(k) % 512 // 64]


def pack_weight(w):
    k, n = w.shape
    w = f64(np.asarray(w, np.float32).astype(ml_dtypes.bfloat16)).reshape(k // 32, 32, n)
    amax = np.abs(w).max(1)
    byte = np.clip(np.where(amax > 0, np.frexp(amax)[1] - 1 + 127 - 7, 1), 1, 254)
    scaled = (w * np.exp2(127.0 - byte)[:, None, :]).reshape(k, n).astype(np.float32)
    words = np.ascontiguousarray(scaled.reshape(k // 512, 128, 4, n).transpose(0, 1, 3, 2)).astype(ml_dtypes.float8_e4m3fn).view(np.uint8)
    return words, np.ascontiguousarray(byte.astype(np.uint8).reshape(k // 512, 16, n))


def unpack_weight(words, scales):
    g, p, n, _ = words.shape
    vals = np.ascontiguousarray(words).view(ml_dtypes.float8_e4m3fn).astype(np.float64) * np.repeat(np.exp2(scales.astype(np.float64) - 127.0), 8, axis=1)[..., None]
    return vals.transpose(0, 1, 3, 2).reshape(g * 512, n)


def silu(v):
    return v / (1.0 + np.exp(-np.maximum(v, -700.0)))


K, T, S, N = 1024, 2048, 1024, 128


def setup_inputs():
    n = np.random.standard_normal
    s = mx_kscale(K)[:, None]
    packed_xT = pack_weight(n((K, T)) * s)
    return {
        "x_words": packed_xT[0],
        "x_scales": packed_xT[1],
        "w1": (n((K, N)) / np.sqrt(K) / s).astype(np.float32),
        "gamma": np.random.uniform(0.5, 1.5, (N, 1)).astype(np.float32),
        "res": n((N, S)).astype(np.float32),
        "offs": striped8(np.stack([np.random.permutation(T)[:S] for _ in range(8)])),
    }


def reference(x_words, x_scales, w1, gamma, res, offs):
    xq = unpack_weight(x_words, x_scales)[np.arange(K)[:, None], runs(offs, K)]
    h = (mxq(f64(w1), 0, "e4m3").T @ xq) + f64(res)
    hn = (h - h.mean(axis=1, keepdims=True)) / np.sqrt(h.var(axis=1, keepdims=True) + 1e-5)
    return silu(f64(gamma) * hn)

@@ -1,0 +1,154 @@
+from contextlib import ExitStack
+
+import concourse.mybir as mybir
+
+K, T, S, N = 1024, 2048, 1024, 128
+FLOPS = 2 * K * S * N
+
+F32 = mybir.dt.float32
+BF16 = mybir.dt.bfloat16
+I32 = mybir.dt.int32
+U32 = mybir.dt.uint32
+U16 = mybir.dt.uint16
+U8 = mybir.dt.uint8
+FP8X4 = mybir.dt.float8_e4m3fn_x4
+ALU = mybir.AluOpType
+ACT = mybir.ActivationFunctionType
+
+P = 128
+PASSES = 2
+EPS = 0.00001
+CHUNKS = ((0, 512), (512, 768), (768, 1024))
+OUT_COLS = 256
+
+
+def tile_picked_phnorm_silu_p_kernel(tc, x_words, x_scales, w1, gamma, res, offs, out):
+    nc = tc.nc
+    with ExitStack() as ctx:
+        keep = ctx.enter_context(tc.tile_pool(name="keep", bufs=1))
+        psum = ctx.enter_context(tc.psum_pool(name="psum", bufs=1))
+
+        offsets = keep.tile([P, S // 16], U16, name="offsets")
+        nc.sync.dma_start(offsets[:], offs)
+
+        gamma_sb = keep.tile([P, 1], F32, name="gamma_sb")
+        nc.sync.dma_start(gamma_sb[:], gamma)
+        w_raw = [keep.tile([P, 4 * N], F32, name="w_raw%d" % z) for z in range(PASSES)]
+        w_rows = w1.rearrange("(z p j) m -> z p (j m)", z=PASSES, j=4)
+        nc.sync.dma_start(w_raw[0][:], w_rows[0])
+
+        scale_table = keep.tile([P, T], U8, name="scale_table", align_bytes=64)
+        nc.vector.memset(scale_table[:].bitcast(I32), 0)
+        nc.sync.dma_start(scale_table[:].bitcast(I32)[0:P:4, :], x_scales.rearrange("z q c -> q z c").bitcast(I32))
+
+        word_table = [keep.tile([P, T], U32, name="word_table%d" % z, align_bytes=64) for z in range(PASSES)]
+        res_sb = keep.tile([P, S], F32, name="res_sb")
+        nc.sync.dma_start(word_table[0][:].bitcast(I32), x_words[0].rearrange("p n t -> p (n t)").bitcast(I32))
+        nc.sync.dma_start(w_raw[1][:], w_rows[1])
+        nc.sync.dma_start(word_table[1][:].bitcast(I32), x_words[1].rearrange("p n t -> p (n t)").bitcast(I32))
+        nc.sync.dma_start(res_sb[:], res)
+
+        minus_half = keep.tile([P, 1], F32, name="minus_half")
+        nc.gpsimd.memset(minus_half[:], -0.5)
+        warm = keep.tile([P, 1], F32, name="warm")
+        nc.scalar.activation(warm[:], minus_half[:], ACT.Silu)
+
+        x_planes = keep.tile([P, PASSES * S], U8, name="x_planes", align_bytes=64)
+        nc.gpsimd.memset(x_planes[:].bitcast(I32), 0)
+
+        picked_scales = keep.tile([P, S], U8, name="picked_scales", align_bytes=64)
+        nc.vector.tensor_copy(picked_scales[:], scale_table[:].indirect(offsets[:]))
+        for q in range(4):
+            nc.scalar.dma_start(
+                x_planes[:].bitcast(I32)[32 * q : 32 * q + 4, :],
+                picked_scales[:].bitcast(I32)[32 * q : 32 * q + 32 : 4, :],
+            )
+
+        w_codes = [keep.tile([P, N], U32, name="w_codes%d" % z, align_bytes=64) for z in range(PASSES)]
+        w_planes = [keep.tile([P, N], U8, name="w_planes%d" % z, align_bytes=64) for z in range(PASSES)]
+
+        def quantise_weights(z):
+            grouped = keep.tile([P, N, 4], BF16, name="grouped%d" % z, align_bytes=64)
+            nc.scalar.copy(grouped[:], w_raw[z][:].rearrange("p (j m) -> p m j", j=4))
+            nc.vector.quantize_mx(
+                out=w_codes[z][:].bitcast(FP8X4), scales=w_planes[z][:], in_=grouped[:].rearrange("p m j -> p (m j)")
+            )
+
+        quantise_weights(0)
+        picked0 = keep.tile([P, S], U32, name="picked0", align_bytes=64)
+        nc.vector.tensor_copy(picked0[:], word_table[0][:].indirect(offsets[:]))
+        quantise_weights(1)
+
+        acc = [psum.tile([P, 512], F32, name="acc%d" % c) for c in range(len(CHUNKS))]
+
+        def product(c, z, picked):
+            a, b = CHUNKS[c]
+            nc.tensor.matmul_mx(
+                out=acc[c][:, 0 : b - a],
+                lhsT=w_codes[z][:].bitcast(FP8X4),
+                lhsT_scale=w_planes[z][:],
+                rhs=picked.bitcast(FP8X4),
+                rhs_scale=x_planes[:, z * S + a : z * S + b],
+                start=(z == 0),
+                stop=(z == PASSES - 1),
+            )
+
+        for c, (a, b) in enumerate(CHUNKS):
+            product(c, 0, picked0[:, a:b])
+
+        h = [keep.tile([P, b - a], F32, name="h%d" % c) for c, (a, b) in enumerate(CHUNKS)]
+        sums = [keep.tile([P, 1], F32, name="sum%d" % c) for c in range(len(CHUNKS))]
+        squares = [keep.tile([P, 1], F32, name="square%d" % c) for c in range(len(CHUNKS))]
+        pivot = keep.tile([P, 1], F32, name="pivot")
+        scratch = keep.tile([P, 512], F32, name="scratch")
+
+        def gather_last_pass(c):
+            a, b = CHUNKS[c]
+            picked = keep.tile([P, b - a], U32, name="picked1_%d" % c, align_bytes=64)
+            nc.vector.tensor_copy(picked[:], word_table[1][:].indirect(offsets[:, a // 16 : b // 16]))
+            product(c, 1, picked[:])
+
+        def add_residual(c):
+            a, b = CHUNKS[c]
+            nc.vector.scalar_tensor_tensor(
+                h[c][:], acc[c][:, 0 : b - a], 1.0, res_sb[:, a:b], ALU.mult, ALU.add, accum_out=sums[c][:]
+            )
+            if c == 0:
+                nc.scalar.activation(pivot[:], sums[0][:], ACT.Copy, scale=-1.0 / (32 * (b - a)))
+            nc.scalar.activation(
+                scratch[:, 0 : b - a], h[c][:], ACT.Square, bias=pivot[:], scale=1.0 / 32, accum_out=squares[c][:]
+            )
+
+        gather_last_pass(0)
+        gather_last_pass(1)
+        add_residual(0)
+        gather_last_pass(2)
+        add_residual(1)
+
+        head_diff = keep.tile([P, 1], F32, name="head_diff")
+        nc.gpsimd.tensor_scalar(head_diff[:], sums[1][:], sums[0][:], 1.0 / S, ALU.subtract, ALU.mult)
+        head_sum = keep.tile([P, 1], F32, name="head_sum")
+        nc.gpsimd.tensor_tensor(head_sum[:], sums[1][:], sums[0][:], ALU.add)
+        head_square = keep.tile([P, 1], F32, name="head_square")
+        nc.gpsimd.tensor_scalar(head_square[:], squares[1][:], squares[0][:], EPS, ALU.add, ALU.add)
+
+        add_residual(2)
+
+        shift_square = keep.tile([P, 1], F32, name="shift_square")
+        nc.scalar.activation(shift_square[:], sums[2][:], ACT.Square, bias=head_diff[:], scale=1.0 / S)
+        variance = keep.tile([P, 1], F32, name="variance")
+        nc.gpsimd.tensor_scalar(variance[:], squares[2][:], shift_square[:], head_square[:], ALU.subtract, ALU.add)
+        inv_std = keep.tile([P, 1], F32, name="inv_std")
+        nc.gpsimd.tensor_tensor(inv_std[:], variance[:], minus_half[:], ALU.pow)
+
+        minus_mean = keep.tile([P, 1], F32, name="minus_mean")
+        nc.vector.tensor_scalar(minus_mean[:], sums[2][:], head_sum[:], -1.0 / S, ALU.add, ALU.mult)
+        for c, (a, b) in enumerate(CHUNKS):
+            for o in range(a, b, OUT_COLS):
+                centred = keep.tile([P, OUT_COLS], F32, name="centred%d" % o)
+                nc.vector.tensor_scalar(
+                    centred[:], h[c][:, o - a : o - a + OUT_COLS], minus_mean[:], gamma_sb[:], ALU.add, ALU.mult
+                )
+                result = keep.tile([P, OUT_COLS], F32, name="result%d" % o)
+                nc.scalar.activation(result[:], centred[:], ACT.Silu, scale=inv_std[:])
+                nc.sync.dma_start(out[:, o : o + OUT_COLS], result[:])

@@ -37,32 +37,36 @@ def tile_picked_phnorm_silu_p_kernel(tc, x_words, x_scales, w1, gamma, res, offs
         w_rows = w1.rearrange("(z p j) m -> z p (j m)", z=PASSES, j=4)
         nc.sync.dma_start(w_raw[0][:], w_rows[0])
 
-        scale_table = keep.tile([P, T], U8, name="scale_table", align_bytes=64)
+        scale_table = keep.tile([P, T], U8, name="scale_table", tag="reused", align_bytes=64)
         nc.vector.memset(scale_table[:].bitcast(I32), 0)
         nc.sync.dma_start(scale_table[:].bitcast(I32)[0:P:4, :], x_scales.rearrange("z q c -> q z c").bitcast(I32))
 
         word_table = [keep.tile([P, T], U32, name="word_table%d" % z, align_bytes=64) for z in range(PASSES)]
-        res_sb = keep.tile([P, S], F32, name="res_sb")
         nc.sync.dma_start(word_table[0][:].bitcast(I32), x_words[0].rearrange("p n t -> p (n t)").bitcast(I32))
         nc.sync.dma_start(w_raw[1][:], w_rows[1])
         nc.sync.dma_start(word_table[1][:].bitcast(I32), x_words[1].rearrange("p n t -> p (n t)").bitcast(I32))
-        nc.sync.dma_start(res_sb[:], res)
 
         minus_half = keep.tile([P, 1], F32, name="minus_half")
-        nc.gpsimd.memset(minus_half[:], -0.5)
+        nc.vector.memset(minus_half[:], -0.5)
         warm = keep.tile([P, 1], F32, name="warm")
         nc.scalar.activation(warm[:], minus_half[:], ACT.Silu)
 
+        warm_pow = keep.tile([P, 1], F32, name="warm_pow")
+        nc.gpsimd.tensor_tensor(warm_pow[:], gamma_sb[:], minus_half[:], ALU.pow)
+
         x_planes = keep.tile([P, PASSES * S], U8, name="x_planes", align_bytes=64)
-        nc.gpsimd.memset(x_planes[:].bitcast(I32), 0)
+        nc.vector.memset(x_planes[:].bitcast(I32), 0)
 
         picked_scales = keep.tile([P, S], U8, name="picked_scales", align_bytes=64)
         nc.vector.tensor_copy(picked_scales[:], scale_table[:].indirect(offsets[:]))
         for q in range(4):
-            nc.scalar.dma_start(
+            nc.sync.dma_start(
                 x_planes[:].bitcast(I32)[32 * q : 32 * q + 4, :],
                 picked_scales[:].bitcast(I32)[32 * q : 32 * q + 32 : 4, :],
             )
+
+        res_sb = keep.tile([P, S], F32, name="res_sb", tag="reused", align_bytes=64)
+        nc.sync.dma_start(res_sb[:], res)
 
         w_codes = [keep.tile([P, N], U32, name="w_codes%d" % z, align_bytes=64) for z in range(PASSES)]
         w_planes = [keep.tile([P, N], U8, name="w_planes%d" % z, align_bytes=64) for z in range(PASSES)]
@@ -97,10 +101,10 @@ def tile_picked_phnorm_silu_p_kernel(tc, x_words, x_scales, w1, gamma, res, offs
             product(c, 0, picked0[:, a:b])
 
         h = [keep.tile([P, b - a], F32, name="h%d" % c) for c, (a, b) in enumerate(CHUNKS)]
-        sums = [keep.tile([P, 1], F32, name="sum%d" % c) for c in range(len(CHUNKS))]
-        squares = [keep.tile([P, 1], F32, name="square%d" % c) for c in range(len(CHUNKS))]
+        sums = keep.tile([P, 3], F32, name="sums")
+        terms = keep.tile([P, 3], F32, name="terms")
         pivot = keep.tile([P, 1], F32, name="pivot")
-        scratch = keep.tile([P, 512], F32, name="scratch")
+        scratch = keep.tile([P, S], F32, name="scratch")
 
         def gather_last_pass(c):
             a, b = CHUNKS[c]
@@ -111,12 +115,12 @@ def tile_picked_phnorm_silu_p_kernel(tc, x_words, x_scales, w1, gamma, res, offs
         def add_residual(c):
             a, b = CHUNKS[c]
             nc.vector.scalar_tensor_tensor(
-                h[c][:], acc[c][:, 0 : b - a], 1.0, res_sb[:, a:b], ALU.mult, ALU.add, accum_out=sums[c][:]
+                h[c][:], acc[c][:, 0 : b - a], 1.0, res_sb[:, a:b], ALU.mult, ALU.add, accum_out=sums[:, c : c + 1]
             )
             if c == 0:
-                nc.scalar.activation(pivot[:], sums[0][:], ACT.Copy, scale=-1.0 / (32 * (b - a)))
+                nc.scalar.activation(pivot[:], sums[:, 0:1], ACT.Copy, scale=-1.0 / (32 * (b - a)))
             nc.scalar.activation(
-                scratch[:, 0 : b - a], h[c][:], ACT.Square, bias=pivot[:], scale=1.0 / 32, accum_out=squares[c][:]
+                scratch[:, a:b], h[c][:], ACT.Square, bias=pivot[:], scale=1.0 / 32, accum_out=terms[:, c : c + 1]
             )
 
         gather_last_pass(0)
@@ -125,24 +129,31 @@ def tile_picked_phnorm_silu_p_kernel(tc, x_words, x_scales, w1, gamma, res, offs
         gather_last_pass(2)
         add_residual(1)
 
+        minus_first = keep.tile([P, 1], F32, name="minus_first")
+        nc.scalar.activation(minus_first[:], sums[:, 0:1], ACT.Copy, scale=-1.0 / S)
         head_diff = keep.tile([P, 1], F32, name="head_diff")
-        nc.gpsimd.tensor_scalar(head_diff[:], sums[1][:], sums[0][:], 1.0 / S, ALU.subtract, ALU.mult)
-        head_sum = keep.tile([P, 1], F32, name="head_sum")
-        nc.gpsimd.tensor_tensor(head_sum[:], sums[1][:], sums[0][:], ALU.add)
+        nc.scalar.activation(head_diff[:], sums[:, 1:2], ACT.Identity, bias=minus_first[:], scale=1.0 / S)
+
         head_square = keep.tile([P, 1], F32, name="head_square")
-        nc.gpsimd.tensor_scalar(head_square[:], squares[1][:], squares[0][:], EPS, ALU.add, ALU.add)
+        nc.gpsimd.tensor_scalar(head_square[:], terms[:, 1:2], terms[:, 0:1], EPS, ALU.add, ALU.add)
 
-        add_residual(2)
-
+        a, b = CHUNKS[2]
+        nc.vector.scalar_tensor_tensor(
+            h[2][:], acc[2][:, 0 : b - a], 1.0, res_sb[:, a:b], ALU.mult, ALU.add, accum_out=sums[:, 2:3]
+        )
         shift_square = keep.tile([P, 1], F32, name="shift_square")
-        nc.scalar.activation(shift_square[:], sums[2][:], ACT.Square, bias=head_diff[:], scale=1.0 / S)
+        nc.scalar.activation(shift_square[:], sums[:, 2:3], ACT.Square, bias=head_diff[:], scale=1.0 / S)
+        nc.scalar.activation(
+            scratch[:, a:b], h[2][:], ACT.Square, bias=pivot[:], scale=1.0 / 32, accum_out=terms[:, 2:3]
+        )
         variance = keep.tile([P, 1], F32, name="variance")
-        nc.gpsimd.tensor_scalar(variance[:], squares[2][:], shift_square[:], head_square[:], ALU.subtract, ALU.add)
+        nc.vector.tensor_scalar(variance[:], terms[:, 2:3], shift_square[:], head_square[:], ALU.subtract, ALU.add)
         inv_std = keep.tile([P, 1], F32, name="inv_std")
         nc.gpsimd.tensor_tensor(inv_std[:], variance[:], minus_half[:], ALU.pow)
 
+        scaled_sums = keep.tile([P, 3], F32, name="scaled_sums")
         minus_mean = keep.tile([P, 1], F32, name="minus_mean")
-        nc.vector.tensor_scalar(minus_mean[:], sums[2][:], head_sum[:], -1.0 / S, ALU.add, ALU.mult)
+        nc.vector.tensor_scalar(scaled_sums[:], sums[:], -1.0 / S, None, ALU.mult, ALU.add, accum_out=minus_mean[:])
         for c, (a, b) in enumerate(CHUNKS):
             for o in range(a, b, OUT_COLS):
                 centred = keep.tile([P, OUT_COLS], F32, name="centred%d" % o)

@@ -18,7 +18,7 @@ ACT = mybir.ActivationFunctionType
 P = 128
 PASSES = 2
 EPS = 0.00001
-CHUNKS = ((0, 512), (512, 768), (768, 1024))
+CHUNKS = ((0, 256), (256, 768), (768, 1024))
 OUT_COLS = 256
 
 
@@ -26,18 +26,18 @@ def tile_picked_phnorm_silu_p_kernel(tc, x_words, x_scales, w1, gamma, res, offs
     nc = tc.nc
     with ExitStack() as ctx:
         keep = ctx.enter_context(tc.tile_pool(name="keep", bufs=1))
+        reused = ctx.enter_context(tc.tile_pool(name="reused", bufs=1))
         psum = ctx.enter_context(tc.psum_pool(name="psum", bufs=1))
 
         offsets = keep.tile([P, S // 16], U16, name="offsets")
         nc.sync.dma_start(offsets[:], offs)
 
-        gamma_sb = keep.tile([P, 1], F32, name="gamma_sb")
-        nc.sync.dma_start(gamma_sb[:], gamma)
         w_raw = [keep.tile([P, 4 * N], F32, name="w_raw%d" % z) for z in range(PASSES)]
         w_rows = w1.rearrange("(z p j) m -> z p (j m)", z=PASSES, j=4)
-        nc.sync.dma_start(w_raw[0][:], w_rows[0])
+        nc.sync.dma_start(w_raw[0][:, 0 : 2 * N], w_rows[0][:, 0 : 2 * N])
+        nc.sync.dma_start(w_raw[0][:, 2 * N : 4 * N], w_rows[0][:, 2 * N : 4 * N])
 
-        scale_table = keep.tile([P, T], U8, name="scale_table", tag="reused", align_bytes=64)
+        scale_table = reused.tile([P, T], U8, name="scale_table", offset=0, align_bytes=64)
         nc.vector.memset(scale_table[:].bitcast(I32), 0)
         nc.sync.dma_start(scale_table[:].bitcast(I32)[0:P:4, :], x_scales.rearrange("z q c -> q z c").bitcast(I32))
 
@@ -48,11 +48,11 @@ def tile_picked_phnorm_silu_p_kernel(tc, x_words, x_scales, w1, gamma, res, offs
 
         minus_half = keep.tile([P, 1], F32, name="minus_half")
         nc.vector.memset(minus_half[:], -0.5)
-        warm = keep.tile([P, 1], F32, name="warm")
-        nc.scalar.activation(warm[:], minus_half[:], ACT.Silu)
 
-        warm_pow = keep.tile([P, 1], F32, name="warm_pow")
-        nc.gpsimd.tensor_tensor(warm_pow[:], gamma_sb[:], minus_half[:], ALU.pow)
+
+        term_weights = keep.tile([P, 5], F32, name="term_weights")
+        nc.vector.memset(term_weights[:, 0:4], 1.0 / S)
+        nc.vector.memset(term_weights[:, 4:5], -1.0)
 
         x_planes = keep.tile([P, PASSES * S], U8, name="x_planes", align_bytes=64)
         nc.vector.memset(x_planes[:].bitcast(I32), 0)
@@ -65,23 +65,25 @@ def tile_picked_phnorm_silu_p_kernel(tc, x_words, x_scales, w1, gamma, res, offs
                 picked_scales[:].bitcast(I32)[32 * q : 32 * q + 32 : 4, :],
             )
 
-        res_sb = keep.tile([P, S], F32, name="res_sb", tag="reused", align_bytes=64)
-        nc.sync.dma_start(res_sb[:], res)
+        split = CHUNKS[0][1]
+        res_first = reused.tile([P, split], F32, name="res_first", offset=64, align_bytes=64)
+        res_rest = reused.tile([P, S - split], F32, name="res_rest", offset=64 + 4 * split, align_bytes=64)
+        nc.sync.dma_start(res_first[:], res[:, 0:split])
+        nc.sync.dma_start(res_rest[:], res[:, split:S])
+        gamma_sb = reused.tile([P, 1], F32, name="gamma_sb", offset=0, align_bytes=64)
+        nc.sync.dma_start(gamma_sb[:], gamma)
 
-        w_codes = [keep.tile([P, N], U32, name="w_codes%d" % z, align_bytes=64) for z in range(PASSES)]
-        w_planes = [keep.tile([P, N], U8, name="w_planes%d" % z, align_bytes=64) for z in range(PASSES)]
-
-        def quantise_weights(z):
-            grouped = keep.tile([P, N, 4], BF16, name="grouped%d" % z, align_bytes=64)
-            nc.scalar.copy(grouped[:], w_raw[z][:].rearrange("p (j m) -> p m j", j=4))
-            nc.vector.quantize_mx(
-                out=w_codes[z][:].bitcast(FP8X4), scales=w_planes[z][:], in_=grouped[:].rearrange("p m j -> p (m j)")
-            )
-
-        quantise_weights(0)
         picked0 = keep.tile([P, S], U32, name="picked0", align_bytes=64)
         nc.vector.tensor_copy(picked0[:], word_table[0][:].indirect(offsets[:]))
-        quantise_weights(1)
+
+        grouped = keep.tile([P, PASSES, N, 4], BF16, name="grouped", align_bytes=64)
+        for z in range(PASSES):
+            nc.scalar.copy(grouped[:, z], w_raw[z][:].rearrange("p (j m) -> p m j", j=4))
+        w_codes = keep.tile([P, PASSES * N], U32, name="w_codes", align_bytes=64)
+        w_planes = keep.tile([P, PASSES * N], U8, name="w_planes", align_bytes=64)
+        nc.vector.quantize_mx(
+            out=w_codes[:].bitcast(FP8X4), scales=w_planes[:], in_=grouped[:].rearrange("p z m j -> p (z m j)")
+        )
 
         acc = [psum.tile([P, 512], F32, name="acc%d" % c) for c in range(len(CHUNKS))]
 
@@ -89,77 +91,71 @@ def tile_picked_phnorm_silu_p_kernel(tc, x_words, x_scales, w1, gamma, res, offs
             a, b = CHUNKS[c]
             nc.tensor.matmul_mx(
                 out=acc[c][:, 0 : b - a],
-                lhsT=w_codes[z][:].bitcast(FP8X4),
-                lhsT_scale=w_planes[z][:],
+                lhsT=w_codes[:, z * N : (z + 1) * N].bitcast(FP8X4),
+                lhsT_scale=w_planes[:, z * N : (z + 1) * N],
                 rhs=picked.bitcast(FP8X4),
                 rhs_scale=x_planes[:, z * S + a : z * S + b],
                 start=(z == 0),
                 stop=(z == PASSES - 1),
             )
 
-        for c, (a, b) in enumerate(CHUNKS):
-            product(c, 0, picked0[:, a:b])
-
-        h = [keep.tile([P, b - a], F32, name="h%d" % c) for c, (a, b) in enumerate(CHUNKS)]
-        sums = keep.tile([P, 3], F32, name="sums")
-        terms = keep.tile([P, 3], F32, name="terms")
-        pivot = keep.tile([P, 1], F32, name="pivot")
-        scratch = keep.tile([P, S], F32, name="scratch")
-
         def gather_last_pass(c):
             a, b = CHUNKS[c]
             picked = keep.tile([P, b - a], U32, name="picked1_%d" % c, align_bytes=64)
             nc.vector.tensor_copy(picked[:], word_table[1][:].indirect(offsets[:, a // 16 : b // 16]))
-            product(c, 1, picked[:])
+            return picked
 
-        def add_residual(c):
-            a, b = CHUNKS[c]
-            nc.vector.scalar_tensor_tensor(
-                h[c][:], acc[c][:, 0 : b - a], 1.0, res_sb[:, a:b], ALU.mult, ALU.add, accum_out=sums[:, c : c + 1]
-            )
-            if c == 0:
-                nc.scalar.activation(pivot[:], sums[:, 0:1], ACT.Copy, scale=-1.0 / (32 * (b - a)))
-            nc.scalar.activation(
-                scratch[:, a:b], h[c][:], ACT.Square, bias=pivot[:], scale=1.0 / 32, accum_out=terms[:, c : c + 1]
-            )
+        picked_a = gather_last_pass(0)
+        product(0, 0, picked0[:, CHUNKS[0][0] : CHUNKS[0][1]])
+        product(0, 1, picked_a[:])
+        picked_b = gather_last_pass(1)
+        product(1, 0, picked0[:, CHUNKS[1][0] : CHUNKS[1][1]])
+        product(2, 0, picked0[:, CHUNKS[2][0] : CHUNKS[2][1]])
+        product(1, 1, picked_b[:])
+        picked_c = gather_last_pass(2)
+        product(2, 1, picked_c[:])
 
-        gather_last_pass(0)
-        gather_last_pass(1)
-        add_residual(0)
-        gather_last_pass(2)
-        add_residual(1)
-
-        minus_first = keep.tile([P, 1], F32, name="minus_first")
-        nc.scalar.activation(minus_first[:], sums[:, 0:1], ACT.Copy, scale=-1.0 / S)
-        head_diff = keep.tile([P, 1], F32, name="head_diff")
-        nc.scalar.activation(head_diff[:], sums[:, 1:2], ACT.Identity, bias=minus_first[:], scale=1.0 / S)
-
-        head_square = keep.tile([P, 1], F32, name="head_square")
-        nc.gpsimd.tensor_scalar(head_square[:], terms[:, 1:2], terms[:, 0:1], EPS, ALU.add, ALU.add)
-
-        a, b = CHUNKS[2]
-        nc.vector.scalar_tensor_tensor(
-            h[2][:], acc[2][:, 0 : b - a], 1.0, res_sb[:, a:b], ALU.mult, ALU.add, accum_out=sums[:, 2:3]
-        )
-        shift_square = keep.tile([P, 1], F32, name="shift_square")
-        nc.scalar.activation(shift_square[:], sums[:, 2:3], ACT.Square, bias=head_diff[:], scale=1.0 / S)
+        res_part = keep.tile([P, 1], F32, name="res_part")
+        minus_pivot = keep.tile([P, 1], F32, name="minus_pivot")
+        summed = keep.tile([P, 2, split], F32, name="summed")
+        nc.scalar.activation(summed[:, 0], res_first[:], ACT.Copy, scale=-1.0 / (split * split), accum_out=res_part[:])
         nc.scalar.activation(
-            scratch[:, a:b], h[2][:], ACT.Square, bias=pivot[:], scale=1.0 / 32, accum_out=terms[:, 2:3]
+            summed[:, 1], acc[0][:, 0:split], ACT.Identity, bias=res_part[:], scale=-1.0 / split, accum_out=minus_pivot[:]
         )
+
+        blocks = S // OUT_COLS
+        shifted = [keep.tile([P, OUT_COLS], F32, name="shifted%d" % i) for i in range(blocks)]
+        sums = keep.tile([P, blocks], F32, name="sums")
+        terms = keep.tile([P, blocks + 1], F32, name="terms")
+        squared = keep.tile([P, S], F32, name="squared")
+        for c, (a, b) in enumerate(CHUNKS):
+            for o in range(a, b, OUT_COLS):
+                i = o // OUT_COLS
+                residual = res_first[:] if o < split else res_rest[:, o - split : o - split + OUT_COLS]
+                nc.vector.scalar_tensor_tensor(
+                    shifted[i][:], acc[c][:, o - a : o - a + OUT_COLS], minus_pivot[:], residual, ALU.add, ALU.add,
+                    accum_out=sums[:, i : i + 1],
+                )
+                nc.scalar.activation(
+                    squared[:, o : o + OUT_COLS], shifted[i][:], ACT.Square, accum_out=terms[:, i : i + 1]
+                )
+
+        scaled_sums = keep.tile([P, blocks], F32, name="scaled_sums")
+        minus_shift = keep.tile([P, 1], F32, name="minus_shift")
+        nc.vector.tensor_scalar(scaled_sums[:], sums[:], -1.0 / S, None, ALU.mult, ALU.add, accum_out=minus_shift[:])
+        nc.scalar.activation(terms[:, blocks : blocks + 1], minus_shift[:], ACT.Square)
+
+        weighted = keep.tile([P, blocks + 1], F32, name="weighted")
         variance = keep.tile([P, 1], F32, name="variance")
-        nc.vector.tensor_scalar(variance[:], terms[:, 2:3], shift_square[:], head_square[:], ALU.subtract, ALU.add)
+        nc.vector.scalar_tensor_tensor(
+            weighted[:], terms[:], EPS / (blocks / S - 1.0), term_weights[:], ALU.add, ALU.mult, accum_out=variance[:]
+        )
         inv_std = keep.tile([P, 1], F32, name="inv_std")
         nc.gpsimd.tensor_tensor(inv_std[:], variance[:], minus_half[:], ALU.pow)
 
-        scaled_sums = keep.tile([P, 3], F32, name="scaled_sums")
-        minus_mean = keep.tile([P, 1], F32, name="minus_mean")
-        nc.vector.tensor_scalar(scaled_sums[:], sums[:], -1.0 / S, None, ALU.mult, ALU.add, accum_out=minus_mean[:])
-        for c, (a, b) in enumerate(CHUNKS):
-            for o in range(a, b, OUT_COLS):
-                centred = keep.tile([P, OUT_COLS], F32, name="centred%d" % o)
-                nc.vector.tensor_scalar(
-                    centred[:], h[c][:, o - a : o - a + OUT_COLS], minus_mean[:], gamma_sb[:], ALU.add, ALU.mult
-                )
-                result = keep.tile([P, OUT_COLS], F32, name="result%d" % o)
-                nc.scalar.activation(result[:], centred[:], ACT.Silu, scale=inv_std[:])
-                nc.sync.dma_start(out[:, o : o + OUT_COLS], result[:])
+        for i in range(blocks):
+            centred = keep.tile([P, OUT_COLS], F32, name="centred%d" % i)
+            nc.vector.tensor_scalar(centred[:], shifted[i][:], minus_shift[:], gamma_sb[:], ALU.add, ALU.mult)
+            result = keep.tile([P, OUT_COLS], F32, name="result%d" % i)
+            nc.scalar.activation(result[:], centred[:], ACT.Silu, scale=inv_std[:])
+            nc.sync.dma_start(out[:, i * OUT_COLS : (i + 1) * OUT_COLS], result[:])

@@ -4,6 +4,7 @@ import concourse.mybir as mybir
 
 K, T, S, N = 1024, 2048, 1024, 128
 FLOPS = 2 * K * S * N
+EPS = 0.00001
 
 F32 = mybir.dt.float32
 BF16 = mybir.dt.bfloat16
@@ -16,10 +17,15 @@ ALU = mybir.AluOpType
 ACT = mybir.ActivationFunctionType
 
 P = 128
-PASSES = 2
-EPS = 0.00001
+PACK = 4
+PASSES = K // (P * PACK)
+LIST_ROWS = 16
+QUADRANT = 32
 CHUNKS = ((0, 256), (256, 768), (768, 1024))
-OUT_COLS = 256
+BLOCK = 256
+BLOCKS = S // BLOCK
+PIVOT_COLS = 64
+GAMMA_SLOT = 64
 
 
 def tile_picked_phnorm_silu_p_kernel(tc, x_words, x_scales, w1, gamma, res, offs, out):
@@ -29,13 +35,13 @@ def tile_picked_phnorm_silu_p_kernel(tc, x_words, x_scales, w1, gamma, res, offs
         reused = ctx.enter_context(tc.tile_pool(name="reused", bufs=1))
         psum = ctx.enter_context(tc.psum_pool(name="psum", bufs=1))
 
-        offsets = keep.tile([P, S // 16], U16, name="offsets")
+        offsets = keep.tile([P, S // LIST_ROWS], U16, name="offsets")
         nc.sync.dma_start(offsets[:], offs)
-
-        w_raw = [keep.tile([P, 4 * N], F32, name="w_raw%d" % z) for z in range(PASSES)]
-        w_rows = w1.rearrange("(z p j) m -> z p (j m)", z=PASSES, j=4)
-        nc.sync.dma_start(w_raw[0][:, 0 : 2 * N], w_rows[0][:, 0 : 2 * N])
-        nc.sync.dma_start(w_raw[0][:, 2 * N : 4 * N], w_rows[0][:, 2 * N : 4 * N])
+        w_raw = [keep.tile([P, PACK * N], F32, name="w_raw%d" % z) for z in range(PASSES)]
+        w_rows = w1.rearrange("(z p t) m -> z p (t m)", z=PASSES, t=PACK)
+        half = PACK * N // 2
+        nc.sync.dma_start(w_raw[0][:, 0:half], w_rows[0][:, 0:half])
+        nc.sync.dma_start(w_raw[0][:, half:], w_rows[0][:, half:])
 
         scale_table = reused.tile([P, T], U8, name="scale_table", offset=0, align_bytes=64)
         nc.vector.memset(scale_table[:].bitcast(I32), 0)
@@ -48,41 +54,43 @@ def tile_picked_phnorm_silu_p_kernel(tc, x_words, x_scales, w1, gamma, res, offs
 
         minus_half = keep.tile([P, 1], F32, name="minus_half")
         nc.vector.memset(minus_half[:], -0.5)
+        term_weights = keep.tile([P, BLOCKS + 1], F32, name="term_weights")
+        nc.vector.memset(term_weights[:, 0:BLOCKS], 1.0 / S)
+        nc.vector.memset(term_weights[:, BLOCKS : BLOCKS + 1], -1.0)
 
-
-        term_weights = keep.tile([P, 5], F32, name="term_weights")
-        nc.vector.memset(term_weights[:, 0:4], 1.0 / S)
-        nc.vector.memset(term_weights[:, 4:5], -1.0)
+        warm_up = keep.tile([P, 1], F32, name="warm_up")
+        nc.scalar.activation(warm_up[:], minus_half[:], ACT.Silu)
 
         x_planes = keep.tile([P, PASSES * S], U8, name="x_planes", align_bytes=64)
         nc.vector.memset(x_planes[:].bitcast(I32), 0)
 
         picked_scales = keep.tile([P, S], U8, name="picked_scales", align_bytes=64)
         nc.vector.tensor_copy(picked_scales[:], scale_table[:].indirect(offsets[:]))
-        for q in range(4):
+        for q in range(P // QUADRANT):
+            base = QUADRANT * q
             nc.sync.dma_start(
-                x_planes[:].bitcast(I32)[32 * q : 32 * q + 4, :],
-                picked_scales[:].bitcast(I32)[32 * q : 32 * q + 32 : 4, :],
+                x_planes[:].bitcast(I32)[base : base + 4, :],
+                picked_scales[:].bitcast(I32)[base : base + QUADRANT : 4, :],
             )
 
         split = CHUNKS[0][1]
-        res_first = reused.tile([P, split], F32, name="res_first", offset=64, align_bytes=64)
-        res_rest = reused.tile([P, S - split], F32, name="res_rest", offset=64 + 4 * split, align_bytes=64)
+        res_first = reused.tile([P, split], F32, name="res_first", offset=GAMMA_SLOT, align_bytes=64)
+        res_rest = reused.tile([P, S - split], F32, name="res_rest", offset=GAMMA_SLOT + 4 * split, align_bytes=64)
         nc.sync.dma_start(res_first[:], res[:, 0:split])
         nc.sync.dma_start(res_rest[:], res[:, split:S])
         gamma_sb = reused.tile([P, 1], F32, name="gamma_sb", offset=0, align_bytes=64)
         nc.sync.dma_start(gamma_sb[:], gamma)
 
-        picked0 = keep.tile([P, S], U32, name="picked0", align_bytes=64)
-        nc.vector.tensor_copy(picked0[:], word_table[0][:].indirect(offsets[:]))
+        picked_first = keep.tile([P, S], U32, name="picked_first", align_bytes=64)
+        nc.vector.tensor_copy(picked_first[:], word_table[0][:].indirect(offsets[:]))
 
-        grouped = keep.tile([P, PASSES, N, 4], BF16, name="grouped", align_bytes=64)
+        grouped = keep.tile([P, PASSES, N, PACK], BF16, name="grouped", align_bytes=64)
         for z in range(PASSES):
-            nc.scalar.copy(grouped[:, z], w_raw[z][:].rearrange("p (j m) -> p m j", j=4))
+            nc.scalar.copy(grouped[:, z], w_raw[z][:].rearrange("p (t m) -> p m t", t=PACK))
         w_codes = keep.tile([P, PASSES * N], U32, name="w_codes", align_bytes=64)
         w_planes = keep.tile([P, PASSES * N], U8, name="w_planes", align_bytes=64)
         nc.vector.quantize_mx(
-            out=w_codes[:].bitcast(FP8X4), scales=w_planes[:], in_=grouped[:].rearrange("p z m j -> p (z m j)")
+            out=w_codes[:].bitcast(FP8X4), scales=w_planes[:], in_=grouped[:].rearrange("p z m t -> p (z m t)")
         )
 
         acc = [psum.tile([P, 512], F32, name="acc%d" % c) for c in range(len(CHUNKS))]
@@ -99,63 +107,68 @@ def tile_picked_phnorm_silu_p_kernel(tc, x_words, x_scales, w1, gamma, res, offs
                 stop=(z == PASSES - 1),
             )
 
-        def gather_last_pass(c):
+        def first_pass(c):
             a, b = CHUNKS[c]
-            picked = keep.tile([P, b - a], U32, name="picked1_%d" % c, align_bytes=64)
-            nc.vector.tensor_copy(picked[:], word_table[1][:].indirect(offsets[:, a // 16 : b // 16]))
+            product(c, 0, picked_first[:, a:b])
+
+        def gather_second_pass(c):
+            a, b = CHUNKS[c]
+            picked = keep.tile([P, b - a], U32, name="picked_second%d" % c, align_bytes=64)
+            nc.vector.tensor_copy(picked[:], word_table[1][:].indirect(offsets[:, a // LIST_ROWS : b // LIST_ROWS]))
             return picked
 
-        picked_a = gather_last_pass(0)
-        product(0, 0, picked0[:, CHUNKS[0][0] : CHUNKS[0][1]])
-        product(0, 1, picked_a[:])
-        picked_b = gather_last_pass(1)
-        product(1, 0, picked0[:, CHUNKS[1][0] : CHUNKS[1][1]])
-        product(2, 0, picked0[:, CHUNKS[2][0] : CHUNKS[2][1]])
-        product(1, 1, picked_b[:])
-        picked_c = gather_last_pass(2)
-        product(2, 1, picked_c[:])
+        picked_head = gather_second_pass(0)
+        first_pass(0)
+        product(0, 1, picked_head[:])
+        picked_middle = gather_second_pass(1)
+        first_pass(1)
+        first_pass(2)
+        product(1, 1, picked_middle[:])
+        picked_tail = gather_second_pass(2)
+        product(2, 1, picked_tail[:])
 
         res_part = keep.tile([P, 1], F32, name="res_part")
         minus_pivot = keep.tile([P, 1], F32, name="minus_pivot")
-        summed = keep.tile([P, 2, split], F32, name="summed")
-        nc.scalar.activation(summed[:, 0], res_first[:], ACT.Copy, scale=-1.0 / (split * split), accum_out=res_part[:])
+        summands = keep.tile([P, 2, PIVOT_COLS], F32, name="summands")
         nc.scalar.activation(
-            summed[:, 1], acc[0][:, 0:split], ACT.Identity, bias=res_part[:], scale=-1.0 / split, accum_out=minus_pivot[:]
+            summands[:, 0], res_first[:, 0:PIVOT_COLS], ACT.Copy,
+            scale=-1.0 / (PIVOT_COLS * PIVOT_COLS), accum_out=res_part[:],
+        )
+        nc.scalar.activation(
+            summands[:, 1], acc[0][:, 0:PIVOT_COLS], ACT.Identity,
+            bias=res_part[:], scale=-1.0 / PIVOT_COLS, accum_out=minus_pivot[:],
         )
 
-        blocks = S // OUT_COLS
-        shifted = [keep.tile([P, OUT_COLS], F32, name="shifted%d" % i) for i in range(blocks)]
-        sums = keep.tile([P, blocks], F32, name="sums")
-        terms = keep.tile([P, blocks + 1], F32, name="terms")
+        shifted = [keep.tile([P, BLOCK], F32, name="shifted%d" % i) for i in range(BLOCKS)]
+        sums = keep.tile([P, BLOCKS], F32, name="sums")
+        terms = keep.tile([P, BLOCKS + 1], F32, name="terms")
         squared = keep.tile([P, S], F32, name="squared")
         for c, (a, b) in enumerate(CHUNKS):
-            for o in range(a, b, OUT_COLS):
-                i = o // OUT_COLS
-                residual = res_first[:] if o < split else res_rest[:, o - split : o - split + OUT_COLS]
+            for o in range(a, b, BLOCK):
+                i = o // BLOCK
+                residual = res_first[:] if o < split else res_rest[:, o - split : o - split + BLOCK]
                 nc.vector.scalar_tensor_tensor(
-                    shifted[i][:], acc[c][:, o - a : o - a + OUT_COLS], minus_pivot[:], residual, ALU.add, ALU.add,
+                    shifted[i][:], acc[c][:, o - a : o - a + BLOCK], minus_pivot[:], residual, ALU.add, ALU.add,
                     accum_out=sums[:, i : i + 1],
                 )
-                nc.scalar.activation(
-                    squared[:, o : o + OUT_COLS], shifted[i][:], ACT.Square, accum_out=terms[:, i : i + 1]
-                )
+                nc.scalar.activation(squared[:, o : o + BLOCK], shifted[i][:], ACT.Square, accum_out=terms[:, i : i + 1])
 
-        scaled_sums = keep.tile([P, blocks], F32, name="scaled_sums")
+        scaled_sums = keep.tile([P, BLOCKS], F32, name="scaled_sums")
         minus_shift = keep.tile([P, 1], F32, name="minus_shift")
         nc.vector.tensor_scalar(scaled_sums[:], sums[:], -1.0 / S, None, ALU.mult, ALU.add, accum_out=minus_shift[:])
-        nc.scalar.activation(terms[:, blocks : blocks + 1], minus_shift[:], ACT.Square)
+        nc.scalar.activation(terms[:, BLOCKS : BLOCKS + 1], minus_shift[:], ACT.Square)
 
-        weighted = keep.tile([P, blocks + 1], F32, name="weighted")
+        weighted = keep.tile([P, BLOCKS + 1], F32, name="weighted")
         variance = keep.tile([P, 1], F32, name="variance")
         nc.vector.scalar_tensor_tensor(
-            weighted[:], terms[:], EPS / (blocks / S - 1.0), term_weights[:], ALU.add, ALU.mult, accum_out=variance[:]
+            weighted[:], terms[:], EPS / (BLOCKS / S - 1.0), term_weights[:], ALU.add, ALU.mult, accum_out=variance[:]
         )
         inv_std = keep.tile([P, 1], F32, name="inv_std")
         nc.gpsimd.tensor_tensor(inv_std[:], variance[:], minus_half[:], ALU.pow)
 
-        for i in range(blocks):
-            centred = keep.tile([P, OUT_COLS], F32, name="centred%d" % i)
+        for i in range(BLOCKS):
+            centred = keep.tile([P, BLOCK], F32, name="centred%d" % i)
             nc.vector.tensor_scalar(centred[:], shifted[i][:], minus_shift[:], gamma_sb[:], ALU.add, ALU.mult)
-            result = keep.tile([P, OUT_COLS], F32, name="result%d" % i)
+            result = keep.tile([P, BLOCK], F32, name="result%d" % i)
             nc.scalar.activation(result[:], centred[:], ACT.Silu, scale=inv_std[:])
-            nc.sync.dma_start(out[:, i * OUT_COLS : (i + 1) * OUT_COLS], result[:])
+            nc.sync.dma_start(out[:, i * BLOCK : (i + 1) * BLOCK], result[:])

from contextlib import ExitStack

import concourse.mybir as mybir

K, T, S, N = 1024, 2048, 1024, 128
FLOPS = 2 * K * S * N
EPS = 0.00001

F32 = mybir.dt.float32
BF16 = mybir.dt.bfloat16
I32 = mybir.dt.int32
U32 = mybir.dt.uint32
U16 = mybir.dt.uint16
U8 = mybir.dt.uint8
FP8X4 = mybir.dt.float8_e4m3fn_x4
ALU = mybir.AluOpType
ACT = mybir.ActivationFunctionType

P = 128
PACK = 4
PASSES = K // (P * PACK)
LIST_ROWS = 16
QUADRANT = 32
CHUNKS = ((0, 256), (256, 768), (768, 1024))
BLOCK = 256
BLOCKS = S // BLOCK
PIVOT_COLS = 64
GAMMA_SLOT = 64


def tile_picked_phnorm_silu_p_kernel(tc, x_words, x_scales, w1, gamma, res, offs, out):
    nc = tc.nc
    with ExitStack() as ctx:
        keep = ctx.enter_context(tc.tile_pool(name="keep", bufs=1))
        reused = ctx.enter_context(tc.tile_pool(name="reused", bufs=1))
        psum = ctx.enter_context(tc.psum_pool(name="psum", bufs=1))

        offsets = keep.tile([P, S // LIST_ROWS], U16, name="offsets")
        nc.sync.dma_start(offsets[:], offs)
        w_raw = [keep.tile([P, PACK * N], F32, name="w_raw%d" % z) for z in range(PASSES)]
        w_rows = w1.rearrange("(z p t) m -> z p (t m)", z=PASSES, t=PACK)
        half = PACK * N // 2
        nc.sync.dma_start(w_raw[0][:, 0:half], w_rows[0][:, 0:half])
        nc.sync.dma_start(w_raw[0][:, half:], w_rows[0][:, half:])

        scale_table = reused.tile([P, T], U8, name="scale_table", offset=0, align_bytes=64)
        nc.vector.memset(scale_table[:].bitcast(I32), 0)
        nc.sync.dma_start(scale_table[:].bitcast(I32)[0:P:4, :], x_scales.rearrange("z q c -> q z c").bitcast(I32))

        word_table = [keep.tile([P, T], U32, name="word_table%d" % z, align_bytes=64) for z in range(PASSES)]
        nc.sync.dma_start(word_table[0][:].bitcast(I32), x_words[0].rearrange("p n t -> p (n t)").bitcast(I32))
        nc.sync.dma_start(w_raw[1][:], w_rows[1])
        nc.sync.dma_start(word_table[1][:].bitcast(I32), x_words[1].rearrange("p n t -> p (n t)").bitcast(I32))

        minus_half = keep.tile([P, 1], F32, name="minus_half")
        nc.vector.memset(minus_half[:], -0.5)
        term_weights = keep.tile([P, BLOCKS + 1], F32, name="term_weights")
        nc.vector.memset(term_weights[:, 0:BLOCKS], 1.0 / S)
        nc.vector.memset(term_weights[:, BLOCKS : BLOCKS + 1], -1.0)

        warm_up = keep.tile([P, 1], F32, name="warm_up")
        nc.scalar.activation(warm_up[:], minus_half[:], ACT.Silu)

        x_planes = keep.tile([P, PASSES * S], U8, name="x_planes", align_bytes=64)
        nc.vector.memset(x_planes[:].bitcast(I32), 0)

        picked_scales = keep.tile([P, S], U8, name="picked_scales", align_bytes=64)
        nc.vector.tensor_copy(picked_scales[:], scale_table[:].indirect(offsets[:]))
        for q in range(P // QUADRANT):
            base = QUADRANT * q
            nc.sync.dma_start(
                x_planes[:].bitcast(I32)[base : base + 4, :],
                picked_scales[:].bitcast(I32)[base : base + QUADRANT : 4, :],
            )

        split = CHUNKS[0][1]
        res_first = reused.tile([P, split], F32, name="res_first", offset=GAMMA_SLOT, align_bytes=64)
        res_rest = reused.tile([P, S - split], F32, name="res_rest", offset=GAMMA_SLOT + 4 * split, align_bytes=64)
        nc.sync.dma_start(res_first[:], res[:, 0:split])
        nc.sync.dma_start(res_rest[:], res[:, split:S])
        gamma_sb = reused.tile([P, 1], F32, name="gamma_sb", offset=0, align_bytes=64)
        nc.sync.dma_start(gamma_sb[:], gamma)

        picked_first = keep.tile([P, S], U32, name="picked_first", align_bytes=64)
        nc.vector.tensor_copy(picked_first[:], word_table[0][:].indirect(offsets[:]))

        grouped = keep.tile([P, PASSES, N, PACK], BF16, name="grouped", align_bytes=64)
        for z in range(PASSES):
            nc.scalar.copy(grouped[:, z], w_raw[z][:].rearrange("p (t m) -> p m t", t=PACK))
        w_codes = keep.tile([P, PASSES * N], U32, name="w_codes", align_bytes=64)
        w_planes = keep.tile([P, PASSES * N], U8, name="w_planes", align_bytes=64)
        nc.vector.quantize_mx(
            out=w_codes[:].bitcast(FP8X4), scales=w_planes[:], in_=grouped[:].rearrange("p z m t -> p (z m t)")
        )

        acc = [psum.tile([P, 512], F32, name="acc%d" % c) for c in range(len(CHUNKS))]

        def product(c, z, picked):
            a, b = CHUNKS[c]
            nc.tensor.matmul_mx(
                out=acc[c][:, 0 : b - a],
                lhsT=w_codes[:, z * N : (z + 1) * N].bitcast(FP8X4),
                lhsT_scale=w_planes[:, z * N : (z + 1) * N],
                rhs=picked.bitcast(FP8X4),
                rhs_scale=x_planes[:, z * S + a : z * S + b],
                start=(z == 0),
                stop=(z == PASSES - 1),
            )

        def first_pass(c):
            a, b = CHUNKS[c]
            product(c, 0, picked_first[:, a:b])

        def gather_second_pass(c):
            a, b = CHUNKS[c]
            picked = keep.tile([P, b - a], U32, name="picked_second%d" % c, align_bytes=64)
            nc.vector.tensor_copy(picked[:], word_table[1][:].indirect(offsets[:, a // LIST_ROWS : b // LIST_ROWS]))
            return picked

        picked_head = gather_second_pass(0)
        first_pass(0)
        product(0, 1, picked_head[:])
        picked_middle = gather_second_pass(1)
        first_pass(1)
        first_pass(2)
        product(1, 1, picked_middle[:])
        picked_tail = gather_second_pass(2)
        product(2, 1, picked_tail[:])

        res_part = keep.tile([P, 1], F32, name="res_part")
        minus_pivot = keep.tile([P, 1], F32, name="minus_pivot")
        summands = keep.tile([P, 2, PIVOT_COLS], F32, name="summands")
        nc.scalar.activation(
            summands[:, 0], res_first[:, 0:PIVOT_COLS], ACT.Copy,
            scale=-1.0 / (PIVOT_COLS * PIVOT_COLS), accum_out=res_part[:],
        )
        nc.scalar.activation(
            summands[:, 1], acc[0][:, 0:PIVOT_COLS], ACT.Identity,
            bias=res_part[:], scale=-1.0 / PIVOT_COLS, accum_out=minus_pivot[:],
        )

        shifted = [keep.tile([P, BLOCK], F32, name="shifted%d" % i) for i in range(BLOCKS)]
        sums = keep.tile([P, BLOCKS], F32, name="sums")
        terms = keep.tile([P, BLOCKS + 1], F32, name="terms")
        squared = keep.tile([P, S], F32, name="squared")
        for c, (a, b) in enumerate(CHUNKS):
            for o in range(a, b, BLOCK):
                i = o // BLOCK
                residual = res_first[:] if o < split else res_rest[:, o - split : o - split + BLOCK]
                nc.vector.scalar_tensor_tensor(
                    shifted[i][:], acc[c][:, o - a : o - a + BLOCK], minus_pivot[:], residual, ALU.add, ALU.add,
                    accum_out=sums[:, i : i + 1],
                )
                nc.scalar.activation(squared[:, o : o + BLOCK], shifted[i][:], ACT.Square, accum_out=terms[:, i : i + 1])

        scaled_sums = keep.tile([P, BLOCKS], F32, name="scaled_sums")
        minus_shift = keep.tile([P, 1], F32, name="minus_shift")
        nc.vector.tensor_scalar(scaled_sums[:], sums[:], -1.0 / S, None, ALU.mult, ALU.add, accum_out=minus_shift[:])
        nc.scalar.activation(terms[:, BLOCKS : BLOCKS + 1], minus_shift[:], ACT.Square)

        weighted = keep.tile([P, BLOCKS + 1], F32, name="weighted")
        variance = keep.tile([P, 1], F32, name="variance")
        nc.vector.scalar_tensor_tensor(
            weighted[:], terms[:], EPS / (BLOCKS / S - 1.0), term_weights[:], ALU.add, ALU.mult, accum_out=variance[:]
        )
        inv_std = keep.tile([P, 1], F32, name="inv_std")
        nc.gpsimd.tensor_tensor(inv_std[:], variance[:], minus_half[:], ALU.pow)

        for i in range(BLOCKS):
            centred = keep.tile([P, BLOCK], F32, name="centred%d" % i)
            nc.vector.tensor_scalar(centred[:], shifted[i][:], minus_shift[:], gamma_sb[:], ALU.add, ALU.mult)
            result = keep.tile([P, BLOCK], F32, name="result%d" % i)
            nc.scalar.activation(result[:], centred[:], ACT.Silu, scale=inv_std[:])
            nc.sync.dma_start(out[:, i * BLOCK : (i + 1) * BLOCK], result[:])
